import numpy as np, ml_dtypes
CORES = [88,96,104,112,120,216,224,232,240,248]
N = 10
import mx_ref
NC, G, MB = 128, 2, 3
C = np.float32(0.019)
BF = ml_dtypes.bfloat16
def cut(t, i, w=512):
    return t[:, w * i:w * i + w]
def tile(rs):
    return np.stack(rs, axis=2).reshape(128, -1).astype(BF)
def layer(w, X):
    out = []
    for i in range(G):
        for t in range(len(X)):
            p = mx_ref.matmul(mx_ref.quantize(cut(w, len(X) * i + t)), X[t])
            z = p if t == 0 else z + p
        out.append(z)
    return out
def act(Z):
    return [np.maximum(s * z, 0) * C for z in Z for s in (1, -1)]
def setup_inputs(rng):
    def f(*shape):
        return mx_ref.flush((rng.standard_normal(shape, dtype=np.float32) * np.exp2(rng.integers(-2, 3, shape[:-1] + (1,)))).astype(BF))
    return {"x": f(N, 128, MB * 4 * NC), "w": f(N, 128, G * 512)}
def setup_inputs_blocks(rng):
    d = setup_inputs(rng)
    for k in ("x",): d[k] = mx_ref.spread(d[k], rng, 4)
    for k in ("w",): d[k] = mx_ref.spread(d[k], rng, 1)
    return d
def setup_inputs_wide(rng):
    d = setup_inputs(rng)
    for k in ("x",): d[k] = mx_ref.flush((d[k].astype(np.float32) * np.exp2(rng.integers(-8, 9, (N, 1, 1))).astype(np.float32)).astype(BF))
    return d
def setup_inputs_zeros(rng):
    d = setup_inputs(rng); v = d["x"].reshape(N, 128, -1, 4).copy()
    v[np.broadcast_to((rng.random((N, 1, v.shape[2], 1)) < 0.33), v.shape)] = 0
    d["x"] = v.reshape(d["x"].shape)
    return d
def reference(x, w):
    y = np.full((N, 128, MB * G * NC), np.nan, np.float32)
    for m in range(MB):
        a = mx_ref.quantize(cut(x[N - 1], m, 4 * NC))
        for s in range(N - 1):
            a = mx_ref.quantize(tile(act(layer(w[s], [a]))))
        Z = layer(w[N - 1], [a])
        for i in range(G):
            y[N - 1][:, NC * (G * m + i):NC * (G * m + i) + NC] = Z[i]
    return {"y": y}

@@ -1,0 +1,132 @@
+import numpy as np
+from concourse.mybir import dt, AluOpType, ActivationFunctionType
+
+N, MB, G, NC = 10, 3, 2, 128
+WORLD = 256
+CS = float(np.float32(0.019))
+K = 8
+PIECES = (0, 1)
+
+SCRATCH = {
+    "xb": ("sbuf", [128, MB * 4 * NC], "bfloat16"),
+    "wb": ("sbuf", [128, G * 512], "bfloat16"),
+    "wq": ("sbuf", [128, G * 128], "float8_e4m3fn_x4"),
+    "ws": ("sbuf", [128, G * 128], "uint8"),
+    "aq": ("sbuf", [128, MB * NC], "float8_e4m3fn_x4"),
+    "asc": ("sbuf", [128, MB * NC], "uint8"),
+    "oq": ("sbuf", [128, MB * NC], "float8_e4m3fn_x4"),
+    "osc": ("sbuf", [128, MB * NC], "uint8"),
+    "h": ("sbuf", [128, MB * 4 * NC], "bfloat16"),
+    "z": ("psum", [128, 512 * G * MB], "float32"),
+    "yb": ("sbuf", [128, MB * G * NC], "float32"),
+}
+SEMAPHORES = (["sent", "wqd", "yst"] + ["wl%d" % i for i in range(G)]
+              + ["%s%d" % (n, m) for m in range(MB) for n in ("xl", "q", "arr", "za", "zb", "r", "yc")])
+
+
+def _pick(topo, a, b, j, n):
+    full = topo.mask(a, b)
+    bits = [e for e in range(full.bit_length()) if (full >> e) & 1]
+    use = bits[j * K:(j + 1) * K] if len(bits) >= n * K else bits[:K]
+    return sum(1 << e for e in use), len(use)
+
+
+def _route(T, topo):
+    cores = [int(c) for c in T.cores]
+    n = len(PIECES)
+    hops = []
+    for k in range(N):
+        src, dst = cores[k - 1], cores[k]
+        if topo.may_write(src, dst):
+            hops.append([[(src, dst) + _pick(topo, src, dst, j, n)] for j in range(n)])
+            continue
+        near = [c for c in range(WORLD) if c not in cores and topo.host(c) == topo.host(src)
+                and topo.chip(c) == topo.chip(src) and topo.may_write(c, dst)]
+        near.sort(key=lambda c: (topo.die(c) != topo.die(src), c))
+        hops.append([[(src, near[j]) + _pick(topo, src, near[j], j, n), (near[j], dst) + _pick(topo, near[j], dst, 0, 1)]
+                     for j in range(n)])
+    return hops
+
+
+def _view(q, s, kind, m):
+    return q[:, NC * m:NC * m + NC].bitcast(dt.uint8) if kind == 0 else s[:, NC * m:NC * m + NC]
+
+
+def _send(g, T, topo, leg, kind, m, made):
+    a, b, mask, cnt = leg
+    rid, pid = topo.addr(b, a)
+    src = _view(T.oq, T.osc, kind, m) if made else _view(T.aq, T.asc, kind, m)
+    g.remote_dma(out_ap=_view(T.aq, T.asc, kind, m), in_ap=src, remote_sem=T.sem["arr%d" % m], local_sem=T.sem.sent,
+                 pid=pid, routing_id=rid, dma_engine_mask=mask)
+    return cnt
+
+
+def rank_program(g, core, T, topo):
+    hops = _route(T, topo)
+    sem = T.sem
+    rank = T.rank_of(core)
+
+    if rank is None:
+        left = 0
+        for legs in hops:
+            for j, kind in enumerate(PIECES):
+                if len(legs[j]) == 2 and legs[j][1][0] == core:
+                    for m in range(MB):
+                        g.wait_ge(sem["arr%d" % m], legs[j][0][3])
+                        left += _send(g, T, topo, legs[j][1], kind, m, False)
+        if left:
+            g.wait_ge(sem.sent, left)
+        return
+
+    last = rank == N - 1
+    tile = lambda t, m: t[:, 512 * m:512 * m + 512]
+    cols = lambda t, m: t[:, NC * m:NC * m + NC]
+
+    if last:
+        for m in range(MB):
+            g.sync.dma_start(tile(T.xb, m), tile(T.x, m)).then_inc(sem["xl%d" % m], 16)
+    for i in range(G):
+        (g.sync if last or i == 0 else g.scalar).dma_start(tile(T.wb, i), tile(T.w, i)).then_inc(sem["wl%d" % i], 16)
+    if last:
+        for m in range(MB):
+            g.vector.wait_ge(sem["xl%d" % m], 16)
+            g.vector.quantize_mx(cols(T.oq, m), cols(T.osc, m), tile(T.xb, m)).then_inc(sem["q%d" % m], 1)
+    for i in range(G):
+        g.vector.wait_ge(sem["wl%d" % i], 16)
+        g.vector.quantize_mx(cols(T.wq, i), cols(T.ws, i), tile(T.wb, i)).then_inc(sem.wqd, 1)
+
+    arrives = sum(legs[-1][3] for legs in hops[rank])
+    g.tensor.wait_ge(sem.wqd, G)
+    for m in range(MB):
+        z = [T.z[:, 512 * (G * m + i):512 * (G * m + i) + NC] for i in range(G)]
+        g.tensor.wait_ge(sem["arr%d" % m], arrives)
+        for i in range(G):
+            g.tensor.matmul_mx(z[i], cols(T.wq, i), cols(T.ws, i), cols(T.aq, m), cols(T.asc, m), True, True
+                               ).then_inc(sem["%s%d" % ("za", m) if i == 0 else "%s%d" % ("zb", m)], 1)
+        if last:
+            g.scalar.wait_ge(sem["za%d" % m], 1)
+            g.scalar.activation(cols(T.yb, G * m), z[0], ActivationFunctionType.Copy).then_inc(sem["yc%d" % m], 1)
+            g.vector.wait_ge(sem["zb%d" % m], 1)
+            g.vector.tensor_copy(cols(T.yb, G * m + 1), z[1]).then_inc(sem["yc%d" % m], 1)
+            g.sync.wait_ge(sem["yc%d" % m], 2)
+            g.sync.dma_start(T.y[:, G * NC * m:G * NC * (m + 1)], T.yb[:, G * NC * m:G * NC * (m + 1)]).then_inc(sem.yst, 16)
+            continue
+        part = lambda b: T.h[:, 512 * m + b:512 * m + 512:4]
+        g.scalar.wait_ge(sem["za%d" % m], 1)
+        g.scalar.activation(part(0), z[0], ActivationFunctionType.Relu, scale=CS).then_inc(sem["r%d" % m], 1)
+        g.scalar.activation(part(1), z[0], ActivationFunctionType.Relu, scale=-CS).then_inc(sem["r%d" % m], 1)
+        g.vector.wait_ge(sem["zb%d" % m], 1)
+        g.vector.tensor_scalar(part(2), z[1], CS, 0.0, AluOpType.mult, AluOpType.max).then_inc(sem["r%d" % m], 1)
+        g.vector.tensor_scalar(part(3), z[1], -CS, 0.0, AluOpType.mult, AluOpType.max).then_inc(sem["r%d" % m], 1)
+        g.vector.wait_ge(sem["r%d" % m], 4)
+        g.vector.quantize_mx(cols(T.oq, m), cols(T.osc, m), tile(T.h, m)).then_inc(sem["q%d" % m], 1)
+    if last:
+        g.sync.wait_ge(sem.yst, 16 * MB)
+
+    out = hops[(rank + 1) % N]
+    left = 0
+    for m in range(MB):
+        g.wait_ge(sem["q%d" % m], 1)
+        for j, kind in enumerate(PIECES):
+            left += _send(g, T, topo, out[j][0], kind, m, True)
+    g.wait_ge(sem.sent, left)

@@ -3,25 +3,31 @@ from concourse.mybir import dt, AluOpType, ActivationFunctionType
 
 N, MB, G, NC = 10, 3, 2, 128
 WORLD = 256
+COLS = MB * NC
+SW = COLS // 2
+WC = G * 128
+BASE = (SW, 0)
 CS = float(np.float32(0.019))
 K = 8
 PIECES = (0, 1)
 
 SCRATCH = {
-    "xb": ("sbuf", [128, MB * 4 * NC], "bfloat16"),
-    "wb": ("sbuf", [128, G * 512], "bfloat16"),
-    "wq": ("sbuf", [128, G * 128], "float8_e4m3fn_x4"),
-    "ws": ("sbuf", [128, G * 128], "uint8"),
-    "aq": ("sbuf", [128, MB * NC], "float8_e4m3fn_x4"),
-    "asc": ("sbuf", [128, MB * NC], "uint8"),
-    "oq": ("sbuf", [128, MB * NC], "float8_e4m3fn_x4"),
-    "osc": ("sbuf", [128, MB * NC], "uint8"),
-    "h": ("sbuf", [128, MB * 4 * NC], "bfloat16"),
-    "z": ("psum", [128, 512 * G * MB], "float32"),
-    "yb": ("sbuf", [128, MB * G * NC], "float32"),
+    "xb": ("sbuf", [128, 4 * COLS], "bfloat16"),
+    "wb": ("sbuf", [128, 4 * WC], "bfloat16"),
+    "wq": ("sbuf", [128, WC], "float8_e4m3fn_x4"),
+    "ws": ("sbuf", [128, WC], "uint8"),
+    "fq": ("sbuf", [128, WC], "float8_e4m3fn_x4"),
+    "fs": ("sbuf", [128, WC], "uint8"),
+    "aq": ("sbuf", [128, 2 * SW], "float8_e4m3fn_x4"),
+    "asc": ("sbuf", [128, 2 * SW], "uint8"),
+    "oq": ("sbuf", [128, 2 * SW], "float8_e4m3fn_x4"),
+    "osc": ("sbuf", [128, 2 * SW], "uint8"),
+    "h": ("sbuf", [128, 2 * 4 * SW], "bfloat16"),
+    "z": ("psum", [128, 512 * G * 2], "float32"),
+    "yb": ("sbuf", [128, G * COLS], "float32"),
 }
-SEMAPHORES = (["sent", "wqd", "yst"] + ["wl%d" % i for i in range(G)]
-              + ["%s%d" % (n, m) for m in range(MB) for n in ("xl", "q", "arr", "za", "zb", "r", "yc")])
+SEMAPHORES = (["sent", "wl", "wqd", "farr", "yst"]
+              + ["%s%d" % (n, u) for u in range(2) for n in ("xl", "q", "arr", "za", "zb", "r", "yc")])
 
 
 def _pick(topo, a, b, j, n):
@@ -31,102 +37,151 @@ def _pick(topo, a, b, j, n):
     return sum(1 << e for e in use), len(use)
 
 
-def _route(T, topo):
-    cores = [int(c) for c in T.cores]
+def _legs(topo, cores, src, dst):
     n = len(PIECES)
-    hops = []
-    for k in range(N):
-        src, dst = cores[k - 1], cores[k]
-        if topo.may_write(src, dst):
-            hops.append([[(src, dst) + _pick(topo, src, dst, j, n)] for j in range(n)])
-            continue
-        near = [c for c in range(WORLD) if c not in cores and topo.host(c) == topo.host(src)
-                and topo.chip(c) == topo.chip(src) and topo.may_write(c, dst)]
-        near.sort(key=lambda c: (topo.die(c) != topo.die(src), c))
-        hops.append([[(src, near[j]) + _pick(topo, src, near[j], j, n), (near[j], dst) + _pick(topo, near[j], dst, 0, 1)]
-                     for j in range(n)])
-    return hops
+    if topo.may_write(src, dst):
+        return [[(src, dst) + _pick(topo, src, dst, j, n)] for j in range(n)]
+    near = [c for c in range(WORLD) if c not in cores and topo.host(c) == topo.host(src)
+            and topo.chip(c) == topo.chip(src) and topo.may_write(c, dst)]
+    near.sort(key=lambda c: (topo.die(c) != topo.die(src), c))
+    return [[(src, near[j]) + _pick(topo, src, near[j], j, n), (near[j], dst) + _pick(topo, near[j], dst, 0, 1)]
+            for j in range(n)]
 
 
-def _view(q, s, kind, m):
-    return q[:, NC * m:NC * m + NC].bitcast(dt.uint8) if kind == 0 else s[:, NC * m:NC * m + NC]
+def _plan(T, topo):
+    cores = [int(c) for c in T.cores]
+    last = N - 1
+    pairs = [(s, s + 1) for s in range(1, last, 2)]
+    home = [[r for r in p if topo.may_write(cores[last], cores[r])][0] for p in pairs]
+    far = [[r for r in p if r != hm][0] for p, hm in zip(pairs, home)]
+    paths = [[last, 0] + far + [last], [last, 0] + home + [last]]
+    ships = []
+    for a, b in pairs:
+        for s, d in ((a, b), (b, a)):
+            ships.append({"src": s, "dst": d, "sb": ("wq", "ws"), "slo": 0, "db": ("fq", "fs"), "dlo": 0, "n": WC,
+                          "sem": "farr", "ready": "wqd"})
+    for hop in range(len(paths[0]) - 1):
+        for t, path in enumerate(paths):
+            s, d = path[hop], path[hop + 1]
+            ss = t if s in (last, 0) else 1
+            ds = t if d in (last, 0) else 0
+            ships.append({"src": s, "dst": d, "sb": ("oq", "osc"), "slo": SW * ss, "db": ("aq", "asc"), "dlo": SW * ds,
+                          "n": SW, "sem": "arr%d" % ds, "ready": "q%d" % ss})
+    for sh in ships:
+        sh["legs"] = _legs(topo, cores, cores[sh["src"]], cores[sh["dst"]])
+    return cores, pairs, ships
 
 
-def _send(g, T, topo, leg, kind, m, made):
+def _view(T, names, kind, lo, n):
+    return T[names[0]][:, lo:lo + n].bitcast(dt.uint8) if kind == 0 else T[names[1]][:, lo:lo + n]
+
+
+def _send(g, T, topo, leg, sh, kind, first):
     a, b, mask, cnt = leg
     rid, pid = topo.addr(b, a)
-    src = _view(T.oq, T.osc, kind, m) if made else _view(T.aq, T.asc, kind, m)
-    g.remote_dma(out_ap=_view(T.aq, T.asc, kind, m), in_ap=src, remote_sem=T.sem["arr%d" % m], local_sem=T.sem.sent,
-                 pid=pid, routing_id=rid, dma_engine_mask=mask)
+    names, lo = (sh["sb"], sh["slo"]) if first else (sh["db"], sh["dlo"])
+    g.remote_dma(out_ap=_view(T, sh["db"], kind, sh["dlo"], sh["n"]), in_ap=_view(T, names, kind, lo, sh["n"]),
+                 remote_sem=T.sem[sh["sem"]], local_sem=T.sem.sent, pid=pid, routing_id=rid, dma_engine_mask=mask)
     return cnt
 
 
+def _ycols(t):
+    runs, lo = [], BASE[t]
+    while lo < BASE[t] + SW:
+        hi = min(BASE[t] + SW, (lo // NC + 1) * NC)
+        for i in range(G):
+            runs.append((lo - BASE[t], i, NC * (G * (lo // NC) + i) + lo % NC, hi - lo))
+        lo = hi
+    return runs
+
+
 def rank_program(g, core, T, topo):
-    hops = _route(T, topo)
+    cores, pairs, ships = _plan(T, topo)
     sem = T.sem
     rank = T.rank_of(core)
+    left = 0
 
     if rank is None:
-        left = 0
-        for legs in hops:
-            for j, kind in enumerate(PIECES):
-                if len(legs[j]) == 2 and legs[j][1][0] == core:
-                    for m in range(MB):
-                        g.wait_ge(sem["arr%d" % m], legs[j][0][3])
-                        left += _send(g, T, topo, legs[j][1], kind, m, False)
+        for sh in ships:
+            for kind in PIECES:
+                legs = sh["legs"][kind]
+                if len(legs) == 2 and legs[1][0] == core:
+                    g.wait_ge(sem[sh["sem"]], legs[0][3])
+                    left += _send(g, T, topo, legs[1], sh, kind, False)
         if left:
             g.wait_ge(sem.sent, left)
         return
 
     last = rank == N - 1
-    tile = lambda t, m: t[:, 512 * m:512 * m + 512]
-    cols = lambda t, m: t[:, NC * m:NC * m + NC]
+    lands = {}
+    for sh in ships:
+        if sh["dst"] == rank:
+            lands[sh["sem"]] = lands.get(sh["sem"], 0) + sum(legs[-1][3] for legs in sh["legs"])
 
     if last:
-        for m in range(MB):
-            g.sync.dma_start(tile(T.xb, m), tile(T.x, m)).then_inc(sem["xl%d" % m], 16)
-    for i in range(G):
-        (g.sync if last or i == 0 else g.scalar).dma_start(tile(T.wb, i), tile(T.w, i)).then_inc(sem["wl%d" % i], 16)
+        for t in range(2):
+            c = slice(4 * BASE[t], 4 * BASE[t] + 4 * SW)
+            g.sync.dma_start(T.xb[:, c], T.x[:, c]).then_inc(sem["xl%d" % t], 16)
+    g.sync.dma_start(T.wb[:], T.w[:]).then_inc(sem.wl, 16)
     if last:
-        for m in range(MB):
-            g.vector.wait_ge(sem["xl%d" % m], 16)
-            g.vector.quantize_mx(cols(T.oq, m), cols(T.osc, m), tile(T.xb, m)).then_inc(sem["q%d" % m], 1)
-    for i in range(G):
-        g.vector.wait_ge(sem["wl%d" % i], 16)
-        g.vector.quantize_mx(cols(T.wq, i), cols(T.ws, i), tile(T.wb, i)).then_inc(sem.wqd, 1)
+        for t in range(2):
+            g.vector.wait_ge(sem["xl%d" % t], 16)
+            g.vector.quantize_mx(T.oq[:, SW * t:SW * t + SW], T.osc[:, SW * t:SW * t + SW],
+                                 T.xb[:, 4 * BASE[t]:4 * BASE[t] + 4 * SW]).then_inc(sem["q%d" % t], 1)
+    g.vector.wait_ge(sem.wl, 16)
+    g.vector.quantize_mx(T.wq[:], T.ws[:], T.wb[:]).then_inc(sem.wqd, 1)
 
-    arrives = sum(legs[-1][3] for legs in hops[rank])
-    g.tensor.wait_ge(sem.wqd, G)
-    for m in range(MB):
-        z = [T.z[:, 512 * (G * m + i):512 * (G * m + i) + NC] for i in range(G)]
-        g.tensor.wait_ge(sem["arr%d" % m], arrives)
+    own = (T.wq, T.ws, "wqd", 1)
+    if rank == 0 or last:
+        units = [(t, T.aq, T.asc, SW * t, "arr%d" % t, lands["arr%d" % t], own) for t in ((1, 0) if last else (0, 1))]
+    else:
+        pair = [p for p in pairs if rank in p][0]
+        other = (T.fq, T.fs, "farr", lands["farr"])
+        units = [(0, T.aq, T.asc, 0, "arr0", lands["arr0"], own if pair[0] == rank else other),
+                 (1, T.oq, T.osc, 0, "q0", 1, own if pair[1] == rank else other)]
+
+    for u, mq, ms, lo, msem, mval, (sq, ss, ssem, sval) in units:
+        zc = [512 * (G * u + i) for i in range(G)]
+        g.tensor.wait_ge(sem[ssem], sval)
+        g.tensor.wait_ge(sem[msem], mval)
         for i in range(G):
-            g.tensor.matmul_mx(z[i], cols(T.wq, i), cols(T.ws, i), cols(T.aq, m), cols(T.asc, m), True, True
-                               ).then_inc(sem["%s%d" % ("za", m) if i == 0 else "%s%d" % ("zb", m)], 1)
+            g.tensor.matmul_mx(T.z[:, zc[i]:zc[i] + SW], sq[:, 128 * i:128 * i + 128], ss[:, 128 * i:128 * i + 128],
+                               mq[:, lo:lo + SW], ms[:, lo:lo + SW], True, True
+                               ).then_inc(sem["%s%d" % ("za" if i == 0 else "zb", u)], 1)
+        g.scalar.wait_ge(sem["za%d" % u], 1)
+        g.vector.wait_ge(sem["zb%d" % u], 1)
         if last:
-            g.scalar.wait_ge(sem["za%d" % m], 1)
-            g.scalar.activation(cols(T.yb, G * m), z[0], ActivationFunctionType.Copy).then_inc(sem["yc%d" % m], 1)
-            g.vector.wait_ge(sem["zb%d" % m], 1)
-            g.vector.tensor_copy(cols(T.yb, G * m + 1), z[1]).then_inc(sem["yc%d" % m], 1)
-            g.sync.wait_ge(sem["yc%d" % m], 2)
-            g.sync.dma_start(T.y[:, G * NC * m:G * NC * (m + 1)], T.yb[:, G * NC * m:G * NC * (m + 1)]).then_inc(sem.yst, 16)
+            for off, i, yc, n in _ycols(u):
+                src, dst = T.z[:, zc[i] + off:zc[i] + off + n], T.yb[:, yc:yc + n]
+                if i == 0:
+                    g.scalar.activation(dst, src, ActivationFunctionType.Copy).then_inc(sem["yc%d" % u], 1)
+                else:
+                    g.vector.tensor_copy(dst, src).then_inc(sem["yc%d" % u], 1)
             continue
-        part = lambda b: T.h[:, 512 * m + b:512 * m + 512:4]
-        g.scalar.wait_ge(sem["za%d" % m], 1)
-        g.scalar.activation(part(0), z[0], ActivationFunctionType.Relu, scale=CS).then_inc(sem["r%d" % m], 1)
-        g.scalar.activation(part(1), z[0], ActivationFunctionType.Relu, scale=-CS).then_inc(sem["r%d" % m], 1)
-        g.vector.wait_ge(sem["zb%d" % m], 1)
-        g.vector.tensor_scalar(part(2), z[1], CS, 0.0, AluOpType.mult, AluOpType.max).then_inc(sem["r%d" % m], 1)
-        g.vector.tensor_scalar(part(3), z[1], -CS, 0.0, AluOpType.mult, AluOpType.max).then_inc(sem["r%d" % m], 1)
-        g.vector.wait_ge(sem["r%d" % m], 4)
-        g.vector.quantize_mx(cols(T.oq, m), cols(T.osc, m), tile(T.h, m)).then_inc(sem["q%d" % m], 1)
-    if last:
-        g.sync.wait_ge(sem.yst, 16 * MB)
+        z = [T.z[:, c:c + SW] for c in zc]
+        part = lambda b: T.h[:, 4 * SW * u + b:4 * SW * (u + 1):4]
+        g.scalar.activation(part(0), z[0], ActivationFunctionType.Relu, scale=CS).then_inc(sem["r%d" % u], 1)
+        g.scalar.activation(part(1), z[0], ActivationFunctionType.Relu, scale=-CS).then_inc(sem["r%d" % u], 1)
+        g.vector.tensor_scalar(part(2), z[1], CS, 0.0, AluOpType.mult, AluOpType.max).then_inc(sem["r%d" % u], 1)
+        g.vector.tensor_scalar(part(3), z[1], -CS, 0.0, AluOpType.mult, AluOpType.max).then_inc(sem["r%d" % u], 1)
+        g.vector.wait_ge(sem["r%d" % u], 4)
+        g.vector.quantize_mx(T.oq[:, SW * u:SW * u + SW], T.osc[:, SW * u:SW * u + SW],
+                             T.h[:, 4 * SW * u:4 * SW * (u + 1)]).then_inc(sem["q%d" % u], 1)
 
-    out = hops[(rank + 1) % N]
-    left = 0
-    for m in range(MB):
-        g.wait_ge(sem["q%d" % m], 1)
-        for j, kind in enumerate(PIECES):
-            left += _send(g, T, topo, out[j][0], kind, m, True)
+    if last:
+        a = min(yc for _, _, yc, n in _ycols(0))
+        b = max(yc + n for _, _, yc, n in _ycols(0))
+        early = [(lo, hi) for lo, hi in ((0, a), (b, G * COLS)) if hi > lo]
+        g.sync.wait_ge(sem.yc1, len(_ycols(1)))
+        for lo, hi in early:
+            g.sync.dma_start(T.y[:, lo:hi], T.yb[:, lo:hi]).then_inc(sem.yst, 16)
+        g.sync.wait_ge(sem.yc0, len(_ycols(0)))
+        g.sync.dma_start(T.y[:, a:b], T.yb[:, a:b]).then_inc(sem.yst, 16)
+        g.sync.wait_ge(sem.yst, 16 * (len(early) + 1))
+
+    for sh in ships:
+        if sh["src"] == rank:
+            g.wait_ge(sem[sh["ready"]], 1)
+            for kind in PIECES:
+                left += _send(g, T, topo, sh["legs"][kind][0], sh, kind, True)
     g.wait_ge(sem.sent, left)

import numpy as np
from concourse.mybir import dt, AluOpType, ActivationFunctionType

N, MB, G, NC = 10, 3, 2, 128
WORLD = 256
COLS = MB * NC
SW = COLS // 2
WC = G * 128
BASE = (SW, 0)
CS = float(np.float32(0.019))
K = 8
PIECES = (0, 1)

SCRATCH = {
    "xb": ("sbuf", [128, 4 * COLS], "bfloat16"),
    "wb": ("sbuf", [128, 4 * WC], "bfloat16"),
    "wq": ("sbuf", [128, WC], "float8_e4m3fn_x4"),
    "ws": ("sbuf", [128, WC], "uint8"),
    "fq": ("sbuf", [128, WC], "float8_e4m3fn_x4"),
    "fs": ("sbuf", [128, WC], "uint8"),
    "aq": ("sbuf", [128, 2 * SW], "float8_e4m3fn_x4"),
    "asc": ("sbuf", [128, 2 * SW], "uint8"),
    "oq": ("sbuf", [128, 2 * SW], "float8_e4m3fn_x4"),
    "osc": ("sbuf", [128, 2 * SW], "uint8"),
    "h": ("sbuf", [128, 2 * 4 * SW], "bfloat16"),
    "z": ("psum", [128, 512 * G * 2], "float32"),
    "yb": ("sbuf", [128, G * COLS], "float32"),
}
SEMAPHORES = (["sent", "wl", "wqd", "farr", "yst"]
              + ["%s%d" % (n, u) for u in range(2) for n in ("xl", "q", "arr", "za", "zb", "r", "yc")])


def _pick(topo, a, b, j, n):
    full = topo.mask(a, b)
    bits = [e for e in range(full.bit_length()) if (full >> e) & 1]
    use = bits[j * K:(j + 1) * K] if len(bits) >= n * K else bits[:K]
    return sum(1 << e for e in use), len(use)


def _legs(topo, cores, src, dst):
    n = len(PIECES)
    if topo.may_write(src, dst):
        return [[(src, dst) + _pick(topo, src, dst, j, n)] for j in range(n)]
    near = [c for c in range(WORLD) if c not in cores and topo.host(c) == topo.host(src)
            and topo.chip(c) == topo.chip(src) and topo.may_write(c, dst)]
    near.sort(key=lambda c: (topo.die(c) != topo.die(src), c))
    return [[(src, near[j]) + _pick(topo, src, near[j], j, n), (near[j], dst) + _pick(topo, near[j], dst, 0, 1)]
            for j in range(n)]


def _plan(T, topo):
    cores = [int(c) for c in T.cores]
    last = N - 1
    pairs = [(s, s + 1) for s in range(1, last, 2)]
    home = [[r for r in p if topo.may_write(cores[last], cores[r])][0] for p in pairs]
    far = [[r for r in p if r != hm][0] for p, hm in zip(pairs, home)]
    paths = [[last, 0] + far + [last], [last, 0] + home + [last]]
    ships = []
    for a, b in pairs:
        for s, d in ((a, b), (b, a)):
            ships.append({"src": s, "dst": d, "sb": ("wq", "ws"), "slo": 0, "db": ("fq", "fs"), "dlo": 0, "n": WC,
                          "sem": "farr", "ready": "wqd"})
    for hop in range(len(paths[0]) - 1):
        for t, path in enumerate(paths):
            s, d = path[hop], path[hop + 1]
            ss = t if s in (last, 0) else 1
            ds = t if d in (last, 0) else 0
            ships.append({"src": s, "dst": d, "sb": ("oq", "osc"), "slo": SW * ss, "db": ("aq", "asc"), "dlo": SW * ds,
                          "n": SW, "sem": "arr%d" % ds, "ready": "q%d" % ss})
    for sh in ships:
        sh["legs"] = _legs(topo, cores, cores[sh["src"]], cores[sh["dst"]])
    return cores, pairs, ships


def _view(T, names, kind, lo, n):
    return T[names[0]][:, lo:lo + n].bitcast(dt.uint8) if kind == 0 else T[names[1]][:, lo:lo + n]


def _send(g, T, topo, leg, sh, kind, first):
    a, b, mask, cnt = leg
    rid, pid = topo.addr(b, a)
    names, lo = (sh["sb"], sh["slo"]) if first else (sh["db"], sh["dlo"])
    g.remote_dma(out_ap=_view(T, sh["db"], kind, sh["dlo"], sh["n"]), in_ap=_view(T, names, kind, lo, sh["n"]),
                 remote_sem=T.sem[sh["sem"]], local_sem=T.sem.sent, pid=pid, routing_id=rid, dma_engine_mask=mask)
    return cnt


def _ycols(t):
    runs, lo = [], BASE[t]
    while lo < BASE[t] + SW:
        hi = min(BASE[t] + SW, (lo // NC + 1) * NC)
        for i in range(G):
            runs.append((lo - BASE[t], i, NC * (G * (lo // NC) + i) + lo % NC, hi - lo))
        lo = hi
    return runs


def rank_program(g, core, T, topo):
    cores, pairs, ships = _plan(T, topo)
    sem = T.sem
    rank = T.rank_of(core)
    left = 0

    if rank is None:
        for sh in ships:
            for kind in PIECES:
                legs = sh["legs"][kind]
                if len(legs) == 2 and legs[1][0] == core:
                    g.wait_ge(sem[sh["sem"]], legs[0][3])
                    left += _send(g, T, topo, legs[1], sh, kind, False)
        if left:
            g.wait_ge(sem.sent, left)
        return

    last = rank == N - 1
    lands = {}
    for sh in ships:
        if sh["dst"] == rank:
            lands[sh["sem"]] = lands.get(sh["sem"], 0) + sum(legs[-1][3] for legs in sh["legs"])

    if last:
        for t in range(2):
            c = slice(4 * BASE[t], 4 * BASE[t] + 4 * SW)
            g.sync.dma_start(T.xb[:, c], T.x[:, c]).then_inc(sem["xl%d" % t], 16)
    g.sync.dma_start(T.wb[:], T.w[:]).then_inc(sem.wl, 16)
    if last:
        for t in range(2):
            g.vector.wait_ge(sem["xl%d" % t], 16)
            g.vector.quantize_mx(T.oq[:, SW * t:SW * t + SW], T.osc[:, SW * t:SW * t + SW],
                                 T.xb[:, 4 * BASE[t]:4 * BASE[t] + 4 * SW]).then_inc(sem["q%d" % t], 1)
    g.vector.wait_ge(sem.wl, 16)
    g.vector.quantize_mx(T.wq[:], T.ws[:], T.wb[:]).then_inc(sem.wqd, 1)

    own = (T.wq, T.ws, "wqd", 1)
    if rank == 0 or last:
        units = [(t, T.aq, T.asc, SW * t, "arr%d" % t, lands["arr%d" % t], own) for t in ((1, 0) if last else (0, 1))]
    else:
        pair = [p for p in pairs if rank in p][0]
        other = (T.fq, T.fs, "farr", lands["farr"])
        units = [(0, T.aq, T.asc, 0, "arr0", lands["arr0"], own if pair[0] == rank else other),
                 (1, T.oq, T.osc, 0, "q0", 1, own if pair[1] == rank else other)]

    for u, mq, ms, lo, msem, mval, (sq, ss, ssem, sval) in units:
        zc = [512 * (G * u + i) for i in range(G)]
        g.tensor.wait_ge(sem[ssem], sval)
        g.tensor.wait_ge(sem[msem], mval)
        for i in range(G):
            g.tensor.matmul_mx(T.z[:, zc[i]:zc[i] + SW], sq[:, 128 * i:128 * i + 128], ss[:, 128 * i:128 * i + 128],
                               mq[:, lo:lo + SW], ms[:, lo:lo + SW], True, True
                               ).then_inc(sem["%s%d" % ("za" if i == 0 else "zb", u)], 1)
        g.scalar.wait_ge(sem["za%d" % u], 1)
        g.vector.wait_ge(sem["zb%d" % u], 1)
        if last:
            for off, i, yc, n in _ycols(u):
                src, dst = T.z[:, zc[i] + off:zc[i] + off + n], T.yb[:, yc:yc + n]
                if i == 0:
                    g.scalar.activation(dst, src, ActivationFunctionType.Copy).then_inc(sem["yc%d" % u], 1)
                else:
                    g.vector.tensor_copy(dst, src).then_inc(sem["yc%d" % u], 1)
            continue
        z = [T.z[:, c:c + SW] for c in zc]
        part = lambda b: T.h[:, 4 * SW * u + b:4 * SW * (u + 1):4]
        g.scalar.activation(part(0), z[0], ActivationFunctionType.Relu, scale=CS).then_inc(sem["r%d" % u], 1)
        g.scalar.activation(part(1), z[0], ActivationFunctionType.Relu, scale=-CS).then_inc(sem["r%d" % u], 1)
        g.vector.tensor_scalar(part(2), z[1], CS, 0.0, AluOpType.mult, AluOpType.max).then_inc(sem["r%d" % u], 1)
        g.vector.tensor_scalar(part(3), z[1], -CS, 0.0, AluOpType.mult, AluOpType.max).then_inc(sem["r%d" % u], 1)
        g.vector.wait_ge(sem["r%d" % u], 4)
        g.vector.quantize_mx(T.oq[:, SW * u:SW * u + SW], T.osc[:, SW * u:SW * u + SW],
                             T.h[:, 4 * SW * u:4 * SW * (u + 1)]).then_inc(sem["q%d" % u], 1)

    if last:
        a = min(yc for _, _, yc, n in _ycols(0))
        b = max(yc + n for _, _, yc, n in _ycols(0))
        early = [(lo, hi) for lo, hi in ((0, a), (b, G * COLS)) if hi > lo]
        g.sync.wait_ge(sem.yc1, len(_ycols(1)))
        for lo, hi in early:
            g.sync.dma_start(T.y[:, lo:hi], T.yb[:, lo:hi]).then_inc(sem.yst, 16)
        g.sync.wait_ge(sem.yc0, len(_ycols(0)))
        g.sync.dma_start(T.y[:, a:b], T.yb[:, a:b]).then_inc(sem.yst, 16)
        g.sync.wait_ge(sem.yst, 16 * (len(early) + 1))

    for sh in ships:
        if sh["src"] == rank:
            g.wait_ge(sem[sh["ready"]], 1)
            for kind in PIECES:
                left += _send(g, T, topo, sh["legs"][kind][0], sh, kind, True)
    g.wait_ge(sem.sent, left)
